import numpy as np
import ml_dtypes

BF16 = ml_dtypes.bfloat16


def bf(x):
    return np.asarray(x, np.float32).astype(BF16)


def f32(x):
    return np.asarray(x, np.float32)


def f64(x):
    return np.asarray(x).astype(np.float64)


def striped(idx):
    return np.tile(idx.reshape(-1, 16).T, (8, 1))


def rows(idx, k):
    return np.tile(idx, (k, 1))


def look(tab, idx):
    return np.take_along_axis(f64(tab), rows(idx, len(tab)), axis=1)


K, S, D, V, N = 128, 256, 4, 64, 256


def setup_inputs():
    return {"tab": f32(np.random.standard_normal((K, S))), "x0": f32(np.random.standard_normal((K, V))), "offs": striped(np.random.permutation(S)[:N])}


def reference(tab, x0, offs):
    idx = offs[:16].T.reshape(-1)
    x = f64(x0)
    for d in range(D):
        x = np.minimum(x, look(tab, idx[d * V:(d + 1) * V]))
    return x

@@ -1,0 +1,30 @@
+import concourse.mybir as mybir
+
+F32 = mybir.dt.float32
+U16 = mybir.dt.uint16
+ENTRIES_PER_COLUMN = 16
+
+
+def tile_lookup_pool_min_out_kernel(tc, tab, x0, offs, out):
+    nc = tc.nc
+    rows, table_columns = tab.shape
+    width = x0.shape[1]
+    list_columns = offs.shape[1]
+    piece_columns = width // ENTRIES_PER_COLUMN
+    neighbours = list_columns // piece_columns
+
+    with tc.tile_pool(name="sbuf", bufs=1) as pool:
+        offsets = pool.tile([rows, list_columns], U16)
+        table = pool.tile([rows, table_columns], F32)
+        centre = pool.tile([rows, width], F32)
+        nc.sync.dma_start(offsets[:], offs)
+        nc.scalar.dma_start(table[:], tab)
+        nc.sync.dma_start(centre[:], x0)
+
+        running = centre
+        for d in range(neighbours):
+            piece = offsets[:, d * piece_columns : (d + 1) * piece_columns]
+            smaller = pool.tile([rows, width], F32, name=f"min{d}")
+            nc.vector.tensor_tensor(smaller[:], table[:].indirect(piece), running[:], mybir.AluOpType.min)
+            running = smaller
+        nc.sync.dma_start(out, running[:])

@@ -7,6 +7,7 @@ ENTRIES_PER_COLUMN = 16
 
 def tile_lookup_pool_min_out_kernel(tc, tab, x0, offs, out):
     nc = tc.nc
+    smallest = mybir.AluOpType.min
     rows, table_columns = tab.shape
     width = x0.shape[1]
     list_columns = offs.shape[1]
@@ -21,10 +22,12 @@ def tile_lookup_pool_min_out_kernel(tc, tab, x0, offs, out):
         nc.scalar.dma_start(table[:], tab)
         nc.sync.dma_start(centre[:], x0)
 
-        running = centre
+        running = [centre, centre]
         for d in range(neighbours):
             piece = offsets[:, d * piece_columns : (d + 1) * piece_columns]
             smaller = pool.tile([rows, width], F32, name=f"min{d}")
-            nc.vector.tensor_tensor(smaller[:], table[:].indirect(piece), running[:], mybir.AluOpType.min)
-            running = smaller
-        nc.sync.dma_start(out, running[:])
+            nc.vector.tensor_tensor(smaller[:], table[:].indirect(piece), running[d % 2][:], smallest)
+            running[d % 2] = smaller
+        pooled = pool.tile([rows, width], F32)
+        nc.vector.tensor_tensor(pooled[:], running[0][:], running[1][:], smallest)
+        nc.sync.dma_start(out, pooled[:])

@@ -15,12 +15,12 @@ def tile_lookup_pool_min_out_kernel(tc, tab, x0, offs, out):
     neighbours = list_columns // piece_columns
 
     with tc.tile_pool(name="sbuf", bufs=1) as pool:
-        offsets = pool.tile([rows, list_columns], U16)
         table = pool.tile([rows, table_columns], F32)
+        offsets = pool.tile([rows, list_columns], U16)
         centre = pool.tile([rows, width], F32)
+        nc.sync.dma_start(table[:], tab)
         nc.sync.dma_start(offsets[:], offs)
-        nc.scalar.dma_start(table[:], tab)
-        nc.sync.dma_start(centre[:], x0)
+        nc.scalar.dma_start(centre[:], x0)
 
         running = [centre, centre]
         for d in range(neighbours):

@@ -16,11 +16,11 @@ def tile_lookup_pool_min_out_kernel(tc, tab, x0, offs, out):
 
     with tc.tile_pool(name="sbuf", bufs=1) as pool:
         table = pool.tile([rows, table_columns], F32)
-        offsets = pool.tile([rows, list_columns], U16)
         centre = pool.tile([rows, width], F32)
+        offsets = pool.tile([rows, list_columns], U16)
         nc.sync.dma_start(table[:], tab)
+        nc.sync.dma_start(centre[:], x0)
         nc.sync.dma_start(offsets[:], offs)
-        nc.scalar.dma_start(centre[:], x0)
 
         running = [centre, centre]
         for d in range(neighbours):

import concourse.mybir as mybir

F32 = mybir.dt.float32
U16 = mybir.dt.uint16
ENTRIES_PER_COLUMN = 16


def tile_lookup_pool_min_out_kernel(tc, tab, x0, offs, out):
    nc = tc.nc
    smallest = mybir.AluOpType.min
    rows, table_columns = tab.shape
    width = x0.shape[1]
    list_columns = offs.shape[1]
    piece_columns = width // ENTRIES_PER_COLUMN
    neighbours = list_columns // piece_columns

    with tc.tile_pool(name="sbuf", bufs=1) as pool:
        table = pool.tile([rows, table_columns], F32)
        centre = pool.tile([rows, width], F32)
        offsets = pool.tile([rows, list_columns], U16)
        nc.sync.dma_start(table[:], tab)
        nc.sync.dma_start(centre[:], x0)
        nc.sync.dma_start(offsets[:], offs)

        running = [centre, centre]
        for d in range(neighbours):
            piece = offsets[:, d * piece_columns : (d + 1) * piece_columns]
            smaller = pool.tile([rows, width], F32, name=f"min{d}")
            nc.vector.tensor_tensor(smaller[:], table[:].indirect(piece), running[d % 2][:], smallest)
            running[d % 2] = smaller
        pooled = pool.tile([rows, width], F32)
        nc.vector.tensor_tensor(pooled[:], running[0][:], running[1][:], smallest)
        nc.sync.dma_start(out, pooled[:])
